import numpy as np
import ml_dtypes


def mxq(x, axis, fmt="e4m3"):
    dtype, down = {"e4m3": (ml_dtypes.float8_e4m3fn, 7), "e5m2": (ml_dtypes.float8_e5m2, 14)}[fmt]
    v = np.moveaxis(np.asarray(x, np.float32).astype(ml_dtypes.bfloat16).astype(np.float64), axis, -1)
    blocks = v.reshape(v.shape[:-1] + (-1, 32))
    amax = np.abs(blocks).max(-1, keepdims=True)
    byte = np.maximum(np.where(amax > 0, np.frexp(amax)[1] - 1 + 127, 0) - down, 1)
    scale = np.exp2(byte - 127.0)
    codes = (blocks / scale).astype(np.float32).astype(dtype).astype(np.float64)
    return np.moveaxis((codes * scale).reshape(v.shape), -1, axis)


WIDE = False


def mx_kscale(k):
    if not WIDE:
        return np.ones(k)
    levels = np.array([10, -10, 5, -5, 0])
    if k % 512:
        return np.exp2(np.random.permutation(np.resize(levels, k // 32))).repeat(32)
    a = np.empty((k // 512, 16))
    for p in range(k // 512):
        a[p, :8] = np.random.permutation(np.resize(levels, 8))
        for g in range(8):
            far = levels[np.abs(levels - a[p, g]) >= 10]
            a[p, g + 8] = far[np.random.randint(len(far))]
    return np.exp2(a.ravel()).repeat(32)


def f64(x):
    return np.asarray(x).astype(np.float64)


def striped(idx):
    return np.tile(idx.reshape(-1, 16).T, (8, 1)).astype(np.uint16)


def unstriped(offs):
    return offs[:16].T.reshape(-1).astype(np.int64)


E2M1 = np.array([0.0, 0.5, 1.0, 1.5, 2.0, 3.0, 4.0, 6.0, -0.0, -0.5, -1.0, -1.5, -2.0, -3.0, -4.0, -6.0])


def pack_weight(w, fmt):
    k, n = w.shape
    w = f64(np.asarray(w, np.float32).astype(ml_dtypes.bfloat16)).reshape(k // 32, 32, n)
    amax = np.abs(w).max(1)
    if fmt == "e4m3":
        byte = np.frexp(amax)[1] - 1 + 127 - 7
    else:
        mant, ex = np.frexp(amax / 6.0)
        byte = np.where(mant > 0.5, ex, ex - 1) + 127
    byte = np.clip(np.where(amax > 0, byte, 1), 1, 254)
    scaled = (w * np.exp2(127.0 - byte)[:, None, :]).reshape(k, n).astype(np.float32)
    by_word = np.ascontiguousarray(scaled.reshape(k // 512, 128, 4, n).transpose(0, 1, 3, 2))
    if fmt == "e4m3":
        words = by_word.astype(ml_dtypes.float8_e4m3fn).view(np.uint8)
    else:
        c = by_word.astype(ml_dtypes.float4_e2m1fn).view(np.uint8) & 0xF
        words = (c[..., 0::2] | (c[..., 1::2] << 4)).reshape(k // 512, 128, 2 * n)
    return np.ascontiguousarray(words), np.ascontiguousarray(byte.astype(np.uint8).reshape(k // 512, 16, n))


def unpack_weight(words, scales, fmt):
    g, _, n = scales.shape
    words = np.ascontiguousarray(words).reshape(g, 128, n, -1)
    if fmt == "e4m3":
        vals = words.view(ml_dtypes.float8_e4m3fn).astype(np.float64)
    else:
        nib = np.empty((g, 128, n, 4), np.uint8)
        nib[..., 0::2] = words & 0xF
        nib[..., 1::2] = words >> 4
        vals = E2M1[nib]
    vals = vals * np.repeat(np.exp2(scales.astype(np.float64) - 127.0), 8, axis=1)[..., None]
    return vals.transpose(0, 1, 3, 2).reshape(g * 512, n)


def gelu(v):
    return 0.5 * v * (1.0 + np.tanh(np.sqrt(2.0 / np.pi) * (v + 0.044715 * v**3)))


K, T, S, H, P, N, P2 = 1024, 4096, 1024, 1024, 512, 512, 256


def setup_inputs():
    n = np.random.standard_normal
    s = mx_kscale(K)[:, None]
    u = mx_kscale(H)[:, None]
    tab_words, tab_scales = pack_weight(n((K, T)) * s, "e4m3")
    w2_words, w2_scales = pack_weight(n((H, N)) / np.sqrt(H) / u, "e2m1")
    return {
        "tab_words": tab_words,
        "tab_scales": tab_scales,
        "offs": striped(np.random.permutation(T)[:S]),
        "pos1": striped(np.random.permutation(S)[:P]),
        "pos2": striped(np.random.permutation(S)[:P]),
        "pos3": striped(np.random.permutation(P)[:P2]),
        "pos4": striped(np.random.permutation(P)[:P2]),
        "w1": (n((K, H)) / np.sqrt(K) / s * u.T).astype(np.float32),
        "gain": np.exp(0.4 * n(H)).astype(np.float32),
        "bed": (0.8 * n((H, S)) * u).astype(np.float32),
        "w2_words": w2_words,
        "w2_scales": w2_scales,
        "w3": (n((H, N)) / np.sqrt(H) / u).astype(np.float32),
    }


def reference(tab_words, tab_scales, offs, pos1, pos2, pos3, pos4, w1, gain, bed, w2_words, w2_scales, w3):
    v = unpack_weight(tab_words, tab_scales, "e4m3")[:, unstriped(offs)]
    w1q = mxq(f64(w1), 0, "e4m3")
    h = f64(gain)[:, None] * (w1q.T @ v) + f64(bed)
    low = np.minimum(h[:, unstriped(pos1)], h[:, unstriped(pos2)])
    lowq = mxq(low, 0, "e4m3")
    w2 = unpack_weight(w2_words, w2_scales, "e2m1")
    w3q = mxq(f64(w3), 0, "e4m3")
    y = np.maximum(w2.T @ lowq, w3q.T @ lowq)
    return np.tanh(y[:, unstriped(pos3)]) + y[:, unstriped(pos4)]

@@ -1,0 +1,285 @@
+from contextlib import ExitStack
+
+import concourse.mybir as mybir
+
+K, T, S, H, J, N, J2 = 1024, 4096, 1024, 1024, 512, 512, 256
+FLOPS = 2 * K * H * S + 2 * 2 * H * N * J
+
+F32 = mybir.dt.float32
+BF16 = mybir.dt.bfloat16
+I32 = mybir.dt.int32
+U32 = mybir.dt.uint32
+U16 = mybir.dt.uint16
+U8 = mybir.dt.uint8
+FP8X4 = mybir.dt.float8_e4m3fn_x4
+FP4X4 = mybir.dt.float4_e2m1fn_x4
+ALU = mybir.AluOpType
+ACT = mybir.ActivationFunctionType
+
+P = 128
+PACK = 4
+PASS = P * PACK
+BANK = 512
+QUADS = 4
+
+
+def tile_list_withering_trough_features_kernel(
+    tc, tab_words, tab_scales, offs, pos1, pos2, pos3, pos4, w1, gain, bed, w2_words, w2_scales, w3, out
+):
+    nc = tc.nc
+    with ExitStack() as ctx:
+        lists = ctx.enter_context(tc.tile_pool(name="lists", bufs=1))
+        keep = ctx.enter_context(tc.tile_pool(name="keep", bufs=1))
+        psum = ctx.enter_context(tc.psum_pool(name="psum", bufs=1))
+
+        def load_list(src, name):
+            tile = lists.tile(list(src.shape), U16, name=name)
+            nc.sync.dma_start(tile[:], src)
+            return tile
+
+        def bank(i):
+            return psum.tile([P, BANK], F32, name="bank%d" % i, tag="bank%d" % i)
+
+        offs_t = load_list(offs, "offs_t")
+
+        tsc = keep.tile([P, T], U8, name="tsc", tag="first_grouped", align_bytes=64)
+        nc.vector.memset(tsc[:].bitcast(I32), 0)
+        w2s = keep.tile([P, 2, N], U8, name="w2s", align_bytes=64)
+        nc.vector.memset(w2s[:].bitcast(I32), 0)
+        for q in range(QUADS):
+            nc.gpsimd.dma_start(
+                tsc[32 * q : 32 * q + 8, :].bitcast(I32), tab_scales[:, 4 * q : 4 * q + 4, :].bitcast(I32)
+            )
+        gain_t = keep.tile([P, 2, PACK], F32, name="gain_t")
+        nc.gpsimd.dma_start(gain_t[:], gain.rearrange("(b p t) -> p b t", p=P, t=PACK))
+        for q in range(QUADS):
+            nc.gpsimd.dma_start(
+                w2s[32 * q : 32 * q + 4, :, :].bitcast(I32),
+                w2_scales[:, 4 * q : 4 * q + 4, :].rearrange("a r n -> r a n").bitcast(I32),
+            )
+
+        tab = []
+        for a in range(2):
+            words = keep.tile([P, T], U32, name="tab%d" % a, align_bytes=64)
+            nc.sync.dma_start(words[:].bitcast(I32), tab_words[a].rearrange("p n t -> p (n t)").bitcast(I32))
+            tab.append(words)
+
+        def load_rows(w, a, c0, width, tag, bufs):
+            raw = keep.tile([P, PACK, width], F32, name="raw", tag=tag, bufs=bufs)
+            nc.sync.dma_start(
+                raw[:], w[a * PASS : (a + 1) * PASS, c0 : c0 + width].rearrange("(p j) c -> p j c", j=PACK)
+            )
+            return raw
+
+        bed_rows = bed.rearrange("(b p t) m -> b t p m", p=P, t=PACK)
+
+        def load_bed(u):
+            tile = keep.tile([P, S], F32, name="bed_t", tag="bed", bufs=6)
+            nc.sync.dma_start(tile[:], bed_rows[u // PACK, u % PACK])
+            return tile
+
+        w1_raw = {}
+        w1_raw[0, 0] = load_rows(w1, 0, 0, PASS, "raw", 4)
+        w1_half = [load_rows(w1, 1, hf * 256, 256, "half", 2) for hf in range(2)]
+        pos1_t = load_list(pos1, "pos1_t")
+        pos2_t = load_list(pos2, "pos2_t")
+        bed_t = {}
+        bed_t[0] = load_bed(0)
+        bed_t[1] = load_bed(1)
+        w1_raw[0, 1] = load_rows(w1, 0, PASS, PASS, "raw", 4)
+        bed_t[2] = load_bed(2)
+        w1_raw[1, 1] = load_rows(w1, 1, PASS, PASS, "raw", 4)
+        bed_t[3] = load_bed(3)
+        bed_t[4] = load_bed(4)
+        w3_raw = [load_rows(w3, 0, 0, N, "raw", 4)]
+        bed_t[5] = load_bed(5)
+        w2w = keep.tile([P, 2, 2 * N], U8, name="w2w", align_bytes=64)
+        nc.sync.dma_start(w2w[:].bitcast(I32), w2_words.rearrange("a p n -> p a n").bitcast(I32))
+        pos3_t = load_list(pos3, "pos3_t")
+        pos4_t = load_list(pos4, "pos4_t")
+
+        vw = []
+        for a in range(2):
+            picked = keep.tile([P, S], U32, name="vw%d" % a, align_bytes=64)
+            nc.vector.tensor_copy(picked[:], tab[a][:].indirect(offs_t[:]))
+            vw.append(picked)
+            if a == 0:
+                vs = keep.tile([P, S], U8, name="vs", align_bytes=64)
+                nc.vector.tensor_copy(vs[:], tsc[:].indirect(offs_t[:]))
+
+        def new_grouped():
+            return keep.tile([P, PASS * PACK], BF16, name="grouped", tag="grouped", bufs=3, align_bytes=64)
+
+        def new_quant(name, width):
+            codes = keep.tile([P, width], U32, name=name + "_c", align_bytes=64)
+            scales = keep.tile([P, width], U8, name=name + "_s", align_bytes=64)
+            return codes, scales
+
+        def quantize(q, grouped, c0, c1):
+            nc.vector.quantize_mx(
+                out=q[0][:, c0:c1].bitcast(FP8X4), scales=q[1][:, c0:c1], in_=grouped[:, PACK * c0 : PACK * c1]
+            )
+
+        def deal_w1(copy, grouped, raw, m0, m1):
+            copy(
+                grouped[:].rearrange("p (t m j) -> p m j t", t=PACK, j=PACK)[:, m0:m1],
+                raw[:].rearrange("p j (m t) -> p m j t", t=PACK),
+            )
+
+        w1q = {}
+        g00 = keep.tile([P, PASS * PACK], BF16, name="g00", tag="first_grouped", align_bytes=64)
+        deal_w1(nc.vector.tensor_copy, g00, w1_raw[0, 0], 0, P)
+        g10 = new_grouped()
+        deal_w1(nc.scalar.copy, g10, w1_half[0], 0, 64)
+        w1q[0, 0] = new_quant("w1q00", PASS)
+        quantize(w1q[0, 0], g00, 0, PASS)
+        deal_w1(nc.vector.tensor_copy, g10, w1_half[1], 64, P)
+        w1q[1, 0] = new_quant("w1q10", PASS)
+        quantize(w1q[1, 0], g10, 0, P)
+        quantize(w1q[1, 0], g10, P, PASS)
+
+        def prepare_w1(a):
+            grouped = new_grouped()
+            deal_w1(nc.scalar.copy, grouped, w1_raw[a, 1], 0, P)
+            w1q[a, 1] = new_quant("w1q%d1" % a, PASS)
+            quantize(w1q[a, 1], grouped, 0, PASS)
+
+        w3q = {}
+
+        def prepare_w3(a):
+            grouped = new_grouped()
+            nc.scalar.copy(
+                grouped[:].rearrange("p (c i j) -> p c j i", i=4, j=PACK),
+                w3_raw[a][:].rearrange("p j (c i) -> p c j i", i=4),
+            )
+            w3q[a] = new_quant("w3q%d" % a, N)
+            quantize(w3q[a], grouped, 0, N)
+
+        def first_stage(u):
+            b, t = divmod(u, PACK)
+            h = keep.tile([P, S], F32, name="h", tag="h", bufs=3)
+            for c in range(2):
+                acc = bank(2 * (u % 2) + c)
+                cols = slice(c * BANK, (c + 1) * BANK)
+                for a in range(2):
+                    nc.tensor.matmul_mx(
+                        out=acc[:],
+                        lhsT=w1q[a, b][0][:, t * P : (t + 1) * P].bitcast(FP8X4),
+                        lhsT_scale=w1q[a, b][1][:, t * P : (t + 1) * P],
+                        rhs=vw[a][:, cols].bitcast(FP8X4),
+                        rhs_scale=vs[4 * a : P, cols],
+                        start=(a == 0),
+                        stop=(a == 1),
+                    )
+                nc.vector.scalar_tensor_tensor(
+                    h[:, cols], acc[:], gain_t[:, b, t : t + 1], bed_t[u][:, cols], ALU.mult, ALU.add
+                )
+            return h
+
+        def pick_ends(ends, u, h):
+            t = u % PACK
+            nc.vector.tensor_copy(ends[0][:, t, :], h[:].indirect(pos1_t[:]))
+            nc.vector.tensor_copy(ends[1][:, t, :], h[:].indirect(pos2_t[:]))
+
+        def lesser(low, ends, j0, j1):
+            nc.vector.tensor_tensor(
+                low[:].rearrange("p (c i t) -> p c t i", i=4, t=PACK)[:, j0 // 4 : j1 // 4],
+                ends[0][:].rearrange("p t (c i) -> p c t i", i=4)[:, j0 // 4 : j1 // 4],
+                ends[1][:].rearrange("p t (c i) -> p c t i", i=4)[:, j0 // 4 : j1 // 4],
+                ALU.min,
+            )
+
+        score = {}
+
+        def second_stage(a, nt, lowq):
+            if a == 0:
+                first = (4 + 2 * nt) % 8
+                score[nt] = (bank(first), bank(first + 1))
+            nc.tensor.matmul_mx(
+                out=score[nt][0][:],
+                lhsT=w2w[:, a, 2 * nt * P : 2 * (nt + 1) * P].bitcast(FP4X4),
+                lhsT_scale=w2s[:, a, nt * P : (nt + 1) * P],
+                rhs=lowq[0][:].bitcast(FP8X4),
+                rhs_scale=lowq[1][:],
+                start=(a == 0),
+                stop=(a == 1),
+            )
+            nc.tensor.matmul_mx(
+                out=score[nt][1][:],
+                lhsT=w3q[a][0][:, nt * P : (nt + 1) * P].bitcast(FP8X4),
+                lhsT_scale=w3q[a][1][:, nt * P : (nt + 1) * P],
+                rhs=lowq[0][:].bitcast(FP8X4),
+                rhs_scale=lowq[1][:],
+                start=(a == 0),
+                stop=(a == 1),
+            )
+
+        lowq = {}
+        h_next = first_stage(0)
+        for b in range(2):
+            ends = [keep.tile([P, PACK, J], F32, name="end%d" % e, tag="end%d" % e, bufs=2) for e in range(2)]
+            for t in range(PACK):
+                u = b * PACK + t
+                h = h_next
+                if u == 0:
+                    prepare_w1(0)
+                    bed_t[6] = load_bed(6)
+                if u == 1:
+                    prepare_w1(1)
+                    bed_t[7] = load_bed(7)
+                    w3_raw.append(load_rows(w3, 1, 0, N, "raw", 4))
+                if u == 3:
+                    prepare_w3(0)
+                if u == 5:
+                    prepare_w3(1)
+                if u + 1 < 2 * PACK:
+                    h_next = first_stage(u + 1)
+                pick_ends(ends, u, h)
+                if u == PACK:
+                    quantize(lowq[0], low0, 0, J)
+                    second_stage(0, 0, lowq[0])
+                    second_stage(0, 1, lowq[0])
+            low = keep.tile([P, J * PACK], BF16, name="low", tag="low", bufs=2, align_bytes=64)
+            lowq[b] = new_quant("lowq%d" % b, J)
+            if b == 0:
+                lesser(low, ends, 0, J)
+                low0 = low
+            else:
+                second_stage(0, 2, lowq[0])
+                second_stage(0, 3, lowq[0])
+                lesser(low, ends, 0, J // 2)
+                lesser(low, ends, J // 2, J)
+                quantize(lowq[1], low, 0, J // 2)
+                quantize(lowq[1], low, J // 2, J)
+
+        for nt in range(N // P):
+            second_stage(1, nt, lowq[1])
+
+        y = {}
+        bent = {}
+
+        def greater(nt):
+            first = keep.tile([P, J], F32, name="first", tag="first", bufs=2)
+            nc.scalar.copy(first[:], score[nt][0][:])
+            y[nt] = keep.tile([P, J], F32, name="y%d" % nt)
+            nc.vector.tensor_tensor(y[nt][:], score[nt][1][:], first[:], ALU.max)
+
+        def earlier(nt):
+            picked = keep.tile([P, J2], F32, name="picked", tag="picked", bufs=2)
+            nc.vector.tensor_copy(picked[:], y[nt][:].indirect(pos3_t[:]))
+            bent[nt] = keep.tile([P, J2], F32, name="bent", tag="bent", bufs=2)
+            nc.scalar.activation(bent[nt][:], picked[:], ACT.Tanh)
+
+        def following(nt):
+            res = keep.tile([P, J2], F32, name="res%d" % nt)
+            nc.vector.tensor_tensor(res[:], y[nt][:].indirect(pos4_t[:]), bent[nt][:], ALU.add)
+            nc.sync.dma_start(out[nt * P : (nt + 1) * P, :], res[:])
+
+        tiles = N // P
+        for step in range(tiles + 2):
+            if step < tiles:
+                greater(step)
+            if 1 <= step <= tiles:
+                earlier(step - 1)
+            if step >= 2:
+                following(step - 2)

@@ -21,6 +21,8 @@ PACK = 4
 PASS = P * PACK
 BANK = 512
 QUADS = 4
+HALF = J // 2
+ON_VECTOR = ((0, 0), (0, 1), (2, 1), (4, 1), (6, 1))
 
 
 def tile_list_withering_trough_features_kernel(
@@ -42,14 +44,17 @@ def tile_list_withering_trough_features_kernel(
 
         offs_t = load_list(offs, "offs_t")
 
-        tsc = keep.tile([P, T], U8, name="tsc", tag="first_grouped", align_bytes=64)
+        tsc = keep.tile([P, T], U8, name="tsc", tag="tsc", align_bytes=64)
         nc.vector.memset(tsc[:].bitcast(I32), 0)
         w2s = keep.tile([P, 2, N], U8, name="w2s", align_bytes=64)
         nc.vector.memset(w2s[:].bitcast(I32), 0)
-        for q in range(QUADS):
-            nc.gpsimd.dma_start(
-                tsc[32 * q : 32 * q + 8, :].bitcast(I32), tab_scales[:, 4 * q : 4 * q + 4, :].bitcast(I32)
-            )
+
+        def load_table_scales(queue):
+            for q in range(QUADS):
+                queue.dma_start(
+                    tsc[32 * q : 32 * q + 8, :].bitcast(I32), tab_scales[:, 4 * q : 4 * q + 4, :].bitcast(I32)
+                )
+
         gain_t = keep.tile([P, 2, PACK], F32, name="gain_t")
         nc.gpsimd.dma_start(gain_t[:], gain.rearrange("(b p t) -> p b t", p=P, t=PACK))
         for q in range(QUADS):
@@ -57,12 +62,6 @@ def tile_list_withering_trough_features_kernel(
                 w2s[32 * q : 32 * q + 4, :, :].bitcast(I32),
                 w2_scales[:, 4 * q : 4 * q + 4, :].rearrange("a r n -> r a n").bitcast(I32),
             )
-
-        tab = []
-        for a in range(2):
-            words = keep.tile([P, T], U32, name="tab%d" % a, align_bytes=64)
-            nc.sync.dma_start(words[:].bitcast(I32), tab_words[a].rearrange("p n t -> p (n t)").bitcast(I32))
-            tab.append(words)
 
         def load_rows(w, a, c0, width, tag, bufs):
             raw = keep.tile([P, PACK, width], F32, name="raw", tag=tag, bufs=bufs)
@@ -74,13 +73,20 @@ def tile_list_withering_trough_features_kernel(
         bed_rows = bed.rearrange("(b p t) m -> b t p m", p=P, t=PACK)
 
         def load_bed(u):
-            tile = keep.tile([P, S], F32, name="bed_t", tag="bed", bufs=6)
+            tile = keep.tile([P, S], F32, name="bed%d" % u, tag="bed%d" % u, align_bytes=64)
             nc.sync.dma_start(tile[:], bed_rows[u // PACK, u % PACK])
             return tile
 
         w1_raw = {}
         w1_raw[0, 0] = load_rows(w1, 0, 0, PASS, "raw", 4)
-        w1_half = [load_rows(w1, 1, hf * 256, 256, "half", 2) for hf in range(2)]
+        load_table_scales(nc.sync)
+        w1_raw[1, 0] = load_rows(w1, 1, 0, PASS, "raw", 4)
+        tab = []
+        for a in range(2):
+            words = keep.tile([P, T], U32, name="tab%d" % a, tag="tab%d" % a, align_bytes=64)
+            nc.sync.dma_start(words[:].bitcast(I32), tab_words[a].rearrange("p n t -> p (n t)").bitcast(I32))
+            tab.append(words)
+
         pos1_t = load_list(pos1, "pos1_t")
         pos2_t = load_list(pos2, "pos2_t")
         bed_t = {}
@@ -90,25 +96,14 @@ def tile_list_withering_trough_features_kernel(
         bed_t[2] = load_bed(2)
         w1_raw[1, 1] = load_rows(w1, 1, PASS, PASS, "raw", 4)
         bed_t[3] = load_bed(3)
-        bed_t[4] = load_bed(4)
         w3_raw = [load_rows(w3, 0, 0, N, "raw", 4)]
+        bed_t[4] = load_bed(4)
+        w3_raw.append(load_rows(w3, 1, 0, N, "raw", 4))
         bed_t[5] = load_bed(5)
-        w2w = keep.tile([P, 2, 2 * N], U8, name="w2w", align_bytes=64)
-        nc.sync.dma_start(w2w[:].bitcast(I32), w2_words.rearrange("a p n -> p a n").bitcast(I32))
-        pos3_t = load_list(pos3, "pos3_t")
-        pos4_t = load_list(pos4, "pos4_t")
+        bed_t[6] = load_bed(6)
 
-        vw = []
-        for a in range(2):
-            picked = keep.tile([P, S], U32, name="vw%d" % a, align_bytes=64)
-            nc.vector.tensor_copy(picked[:], tab[a][:].indirect(offs_t[:]))
-            vw.append(picked)
-            if a == 0:
-                vs = keep.tile([P, S], U8, name="vs", align_bytes=64)
-                nc.vector.tensor_copy(vs[:], tsc[:].indirect(offs_t[:]))
-
-        def new_grouped():
-            return keep.tile([P, PASS * PACK], BF16, name="grouped", tag="grouped", bufs=3, align_bytes=64)
+        def new_grouped(name, tag):
+            return keep.tile([P, 2, PASS * PACK], BF16, name=name, tag=tag, align_bytes=64)
 
         def new_quant(name, width):
             codes = keep.tile([P, width], U32, name=name + "_c", align_bytes=64)
@@ -120,66 +115,78 @@ def tile_list_withering_trough_features_kernel(
                 out=q[0][:, c0:c1].bitcast(FP8X4), scales=q[1][:, c0:c1], in_=grouped[:, PACK * c0 : PACK * c1]
             )
 
-        def deal_w1(copy, grouped, raw, m0, m1):
+        def deal_w1(copy, grouped, raw, m0, m1, r0):
             copy(
-                grouped[:].rearrange("p (t m j) -> p m j t", t=PACK, j=PACK)[:, m0:m1],
-                raw[:].rearrange("p j (m t) -> p m j t", t=PACK),
+                grouped.rearrange("p (t m j) -> p m j t", t=PACK, j=PACK)[:, m0:m1],
+                raw[:].rearrange("p j (m t) -> p m j t", t=PACK)[:, r0 : r0 + m1 - m0],
             )
 
-        w1q = {}
-        g00 = keep.tile([P, PASS * PACK], BF16, name="g00", tag="first_grouped", align_bytes=64)
-        deal_w1(nc.vector.tensor_copy, g00, w1_raw[0, 0], 0, P)
-        g10 = new_grouped()
-        deal_w1(nc.scalar.copy, g10, w1_half[0], 0, 64)
-        w1q[0, 0] = new_quant("w1q00", PASS)
-        quantize(w1q[0, 0], g00, 0, PASS)
-        deal_w1(nc.vector.tensor_copy, g10, w1_half[1], 64, P)
-        w1q[1, 0] = new_quant("w1q10", PASS)
-        quantize(w1q[1, 0], g10, 0, P)
-        quantize(w1q[1, 0], g10, P, PASS)
+        def flat(grouped):
+            return grouped[:].rearrange("p a c -> p (a c)")
 
-        def prepare_w1(a):
-            grouped = new_grouped()
-            deal_w1(nc.scalar.copy, grouped, w1_raw[a, 1], 0, P)
-            w1q[a, 1] = new_quant("w1q%d1" % a, PASS)
-            quantize(w1q[a, 1], grouped, 0, PASS)
-
-        w3q = {}
-
-        def prepare_w3(a):
-            grouped = new_grouped()
-            nc.scalar.copy(
-                grouped[:].rearrange("p (c i j) -> p c j i", i=4, j=PACK),
-                w3_raw[a][:].rearrange("p j (c i) -> p c j i", i=4),
+        w1q = [new_quant("w1q0", 2 * PASS), new_quant("w1q1", 2 * PASS)]
+        g0 = new_grouped("g0", "g0")
+        vs = keep.tile([P, S], U8, name="vs", align_bytes=64)
+        nc.vector.tensor_copy(vs[:], tsc[:].indirect(offs_t[:]))
+        for a in range(2):
+            deal_w1(nc.scalar.copy, g0[:, a, :], w1_raw[a, 0], 0, P, 0)
+            quantize(w1q[0], flat(g0), a * PASS, (a + 1) * PASS)
+        vw = keep.tile([P, 2, S], U32, name="vw", tag="tsc", align_bytes=64)
+        nc.vector.tensor_copy(vw[:, 0, :], tab[0][:].indirect(offs_t[:]))
+        for c in range(2):
+            nc.vector.tensor_copy(
+                vw[:, 1, c * BANK : (c + 1) * BANK], tab[1][:].indirect(offs_t[:, c * 32 : (c + 1) * 32])
             )
-            w3q[a] = new_quant("w3q%d" % a, N)
-            quantize(w3q[a], grouped, 0, N)
+
+        bed_t[7] = load_bed(7)
+        w2w = keep.tile([P, 2, 2 * N], U8, name="w2w", align_bytes=64)
+        nc.sync.dma_start(w2w[:].bitcast(I32), w2_words.rearrange("a p n -> p a n").bitcast(I32))
+        pos3_t = load_list(pos3, "pos3_t")
+        pos4_t = load_list(pos4, "pos4_t")
+
+        acc = {}
+        h = {}
+
+        def first_pass(u, c, a):
+            b, t = divmod(u, PACK)
+            if a == 0:
+                acc[u, c] = bank(2 * t + c)
+            cols = slice(c * BANK, (c + 1) * BANK)
+            rows = slice(a * PASS + t * P, a * PASS + (t + 1) * P)
+            nc.tensor.matmul_mx(
+                out=acc[u, c][:],
+                lhsT=w1q[b][0][:, rows].bitcast(FP8X4),
+                lhsT_scale=w1q[b][1][:, rows],
+                rhs=vw[:, a, cols].bitcast(FP8X4),
+                rhs_scale=vs[4 * a : P, cols],
+                start=(a == 0),
+                stop=(a == 1),
+            )
+
+        def readings(u, c):
+            b, t = divmod(u, PACK)
+            if c == 0:
+                h[u] = keep.tile([P, S], F32, name="h", tag="h", bufs=4)
+            cols = slice(c * BANK, (c + 1) * BANK)
+            if (u, c) in ON_VECTOR:
+                nc.vector.scalar_tensor_tensor(
+                    h[u][:, cols], acc[u, c][:], gain_t[:, b, t : t + 1], bed_t[u][:, cols], ALU.mult, ALU.add
+                )
+            else:
+                gained = keep.tile([P, BANK], F32, name="gained", tag="gained", bufs=4)
+                nc.scalar.activation(gained[:], acc[u, c][:], ACT.Copy, scale=gain_t[:, b, t : t + 1])
+                nc.gpsimd.tensor_tensor(h[u][:, cols], gained[:], bed_t[u][:, cols], ALU.add)
 
         def first_stage(u):
-            b, t = divmod(u, PACK)
-            h = keep.tile([P, S], F32, name="h", tag="h", bufs=3)
             for c in range(2):
-                acc = bank(2 * (u % 2) + c)
-                cols = slice(c * BANK, (c + 1) * BANK)
-                for a in range(2):
-                    nc.tensor.matmul_mx(
-                        out=acc[:],
-                        lhsT=w1q[a, b][0][:, t * P : (t + 1) * P].bitcast(FP8X4),
-                        lhsT_scale=w1q[a, b][1][:, t * P : (t + 1) * P],
-                        rhs=vw[a][:, cols].bitcast(FP8X4),
-                        rhs_scale=vs[4 * a : P, cols],
-                        start=(a == 0),
-                        stop=(a == 1),
-                    )
-                nc.vector.scalar_tensor_tensor(
-                    h[:, cols], acc[:], gain_t[:, b, t : t + 1], bed_t[u][:, cols], ALU.mult, ALU.add
-                )
-            return h
+                if u >= PACK:
+                    first_pass(u, c, 0)
+                first_pass(u, c, 1)
+                readings(u, c)
 
-        def pick_ends(ends, u, h):
-            t = u % PACK
-            nc.vector.tensor_copy(ends[0][:, t, :], h[:].indirect(pos1_t[:]))
-            nc.vector.tensor_copy(ends[1][:, t, :], h[:].indirect(pos2_t[:]))
+        def pick_end(ends, e, u, h, j0, j1):
+            pos = (pos1_t, pos2_t)[e]
+            nc.vector.tensor_copy(ends[e][:, u % PACK, j0:j1], h[:].indirect(pos[:, j0 // 16 : j1 // 16]))
 
         def lesser(low, ends, j0, j1):
             nc.vector.tensor_tensor(
@@ -190,79 +197,101 @@ def tile_list_withering_trough_features_kernel(
             )
 
         score = {}
+        w3q = new_quant("w3q", 2 * N)
 
-        def second_stage(a, nt, lowq):
+        def second_stage(a, nt, hf, lowq):
             if a == 0:
-                first = (4 + 2 * nt) % 8
-                score[nt] = (bank(first), bank(first + 1))
+                score[nt, hf] = bank(2 * nt + hf)
+            cols = slice(hf * HALF, (hf + 1) * HALF)
             nc.tensor.matmul_mx(
-                out=score[nt][0][:],
+                out=score[nt, hf][:, 0:HALF],
                 lhsT=w2w[:, a, 2 * nt * P : 2 * (nt + 1) * P].bitcast(FP4X4),
                 lhsT_scale=w2s[:, a, nt * P : (nt + 1) * P],
-                rhs=lowq[0][:].bitcast(FP8X4),
-                rhs_scale=lowq[1][:],
+                rhs=lowq[0][:, cols].bitcast(FP8X4),
+                rhs_scale=lowq[1][:, cols],
                 start=(a == 0),
-                stop=(a == 1),
+                stop=False,
             )
+            rows = slice(a * N + nt * P, a * N + (nt + 1) * P)
             nc.tensor.matmul_mx(
-                out=score[nt][1][:],
-                lhsT=w3q[a][0][:, nt * P : (nt + 1) * P].bitcast(FP8X4),
-                lhsT_scale=w3q[a][1][:, nt * P : (nt + 1) * P],
-                rhs=lowq[0][:].bitcast(FP8X4),
-                rhs_scale=lowq[1][:],
-                start=(a == 0),
+                out=score[nt, hf][:, HALF:J],
+                lhsT=w3q[0][:, rows].bitcast(FP8X4),
+                lhsT_scale=w3q[1][:, rows],
+                rhs=lowq[0][:, cols].bitcast(FP8X4),
+                rhs_scale=lowq[1][:, cols],
+                start=False,
                 stop=(a == 1),
             )
 
-        lowq = {}
-        h_next = first_stage(0)
-        for b in range(2):
-            ends = [keep.tile([P, PACK, J], F32, name="end%d" % e, tag="end%d" % e, bufs=2) for e in range(2)]
-            for t in range(PACK):
-                u = b * PACK + t
-                h = h_next
-                if u == 0:
-                    prepare_w1(0)
-                    bed_t[6] = load_bed(6)
-                if u == 1:
-                    prepare_w1(1)
-                    bed_t[7] = load_bed(7)
-                    w3_raw.append(load_rows(w3, 1, 0, N, "raw", 4))
-                if u == 3:
-                    prepare_w3(0)
-                if u == 5:
-                    prepare_w3(1)
-                if u + 1 < 2 * PACK:
-                    h_next = first_stage(u + 1)
-                pick_ends(ends, u, h)
-                if u == PACK:
-                    quantize(lowq[0], low0, 0, J)
-                    second_stage(0, 0, lowq[0])
-                    second_stage(0, 1, lowq[0])
-            low = keep.tile([P, J * PACK], BF16, name="low", tag="low", bufs=2, align_bytes=64)
-            lowq[b] = new_quant("lowq%d" % b, J)
-            if b == 0:
-                lesser(low, ends, 0, J)
-                low0 = low
-            else:
-                second_stage(0, 2, lowq[0])
-                second_stage(0, 3, lowq[0])
-                lesser(low, ends, 0, J // 2)
-                lesser(low, ends, J // 2, J)
-                quantize(lowq[1], low, 0, J // 2)
-                quantize(lowq[1], low, J // 2, J)
+        def new_ends():
+            return [keep.tile([P, PACK, J], F32, name="end%d" % e, tag="end%d" % e, bufs=2) for e in range(2)]
 
-        for nt in range(N // P):
-            second_stage(1, nt, lowq[1])
+        def pick_both(ends, u, h):
+            pick_end(ends, 0, u, h, 0, J)
+            pick_end(ends, 1, u, h, 0, J)
 
-        y = {}
+        tiles = N // P
+        lowq = [new_quant("lowq0", J), new_quant("lowq1", J)]
+        for u in range(PACK):
+            for c in range(2):
+                first_pass(u, c, 0)
+        for c in range(2):
+            for u in range(2):
+                first_pass(u, c, 1)
+                readings(u, c)
+        ends = new_ends()
+        pick_both(ends, 0, h[0])
+        first_stage(2)
+        g1 = new_grouped("g1", "bed0")
+        for hf in range(2):
+            deal_w1(nc.scalar.copy, g1[:, 0, :], w1_raw[0, 1], 64 * hf, 64 * (hf + 1), 64 * hf)
+        pick_both(ends, 1, h[1])
+        first_stage(3)
+        for hf in range(2):
+            deal_w1(nc.scalar.copy, g1[:, 1, :], w1_raw[1, 1], 64 * hf, 64 * (hf + 1), 64 * hf)
+        quantize(w1q[1], flat(g1), 0, 2 * PASS)
+        pick_both(ends, 2, h[2])
+        first_stage(4)
+        pick_both(ends, 3, h[3])
+        first_stage(5)
+        low = keep.tile([P, J * PACK], BF16, name="low", tag="low", bufs=2, align_bytes=64)
+        lesser(low, ends, 0, J)
+        ends = new_ends()
+        pick_both(ends, 4, h[4])
+        quantize(lowq[0], low, 0, J)
+        first_stage(6)
+        pick_both(ends, 5, h[5])
+        g3 = new_grouped("g3", "tab0")
+        for a in range(2):
+            for hf in range(2):
+                nc.scalar.copy(
+                    g3[:, a, :].rearrange("p (c i j) -> p c j i", i=4, j=PACK)[:, 64 * hf : 64 * (hf + 1)],
+                    w3_raw[a][:].rearrange("p j (c i) -> p c j i", i=4)[:, 64 * hf : 64 * (hf + 1)],
+                )
+        quantize(w3q, flat(g3), 0, 2 * N)
+        first_stage(7)
+        pick_both(ends, 6, h[6])
+        for nt in range(tiles):
+            for hf in range(2):
+                second_stage(0, nt, hf, lowq[0])
+        low = keep.tile([P, J * PACK], BF16, name="low", tag="low", bufs=2, align_bytes=64)
+        pick_end(ends, 0, 7, h[7], 0, HALF)
+        pick_end(ends, 1, 7, h[7], 0, HALF)
+        pick_end(ends, 0, 7, h[7], HALF, J)
+        lesser(low, ends, 0, HALF)
+        pick_end(ends, 1, 7, h[7], HALF, J)
+        quantize(lowq[1], low, 0, HALF)
+        lesser(low, ends, HALF, J)
+        quantize(lowq[1], low, HALF, J)
+
+        y = [keep.tile([P, J], F32, name="y%d" % nt) for nt in range(tiles)]
         bent = {}
 
-        def greater(nt):
-            first = keep.tile([P, J], F32, name="first", tag="first", bufs=2)
-            nc.scalar.copy(first[:], score[nt][0][:])
-            y[nt] = keep.tile([P, J], F32, name="y%d" % nt)
-            nc.vector.tensor_tensor(y[nt][:], score[nt][1][:], first[:], ALU.max)
+        def greater(nt, hf):
+            second_stage(1, nt, hf, lowq[1])
+            first = keep.tile([P, HALF], F32, name="first", tag="first", bufs=4)
+            nc.scalar.copy(first[:], score[nt, hf][:, 0:HALF])
+            nc.vector.tensor_tensor(y[nt][:, hf * HALF : (hf + 1) * HALF], score[nt, hf][:, HALF:J], first[:], ALU.max)
 
         def earlier(nt):
             picked = keep.tile([P, J2], F32, name="picked", tag="picked", bufs=2)
@@ -275,10 +304,13 @@ def tile_list_withering_trough_features_kernel(
             nc.vector.tensor_tensor(res[:], y[nt][:].indirect(pos4_t[:]), bent[nt][:], ALU.add)
             nc.sync.dma_start(out[nt * P : (nt + 1) * P, :], res[:])
 
-        tiles = N // P
+        greater(0, 0)
+        greater(1, 0)
         for step in range(tiles + 2):
             if step < tiles:
-                greater(step)
+                greater(step, 1)
+            if step + 2 < tiles:
+                greater(step + 2, 0)
             if 1 <= step <= tiles:
                 earlier(step - 1)
             if step >= 2:

from contextlib import ExitStack

import concourse.mybir as mybir

K, T, S, H, J, N, J2 = 1024, 4096, 1024, 1024, 512, 512, 256
FLOPS = 2 * K * H * S + 2 * 2 * H * N * J

F32 = mybir.dt.float32
BF16 = mybir.dt.bfloat16
I32 = mybir.dt.int32
U32 = mybir.dt.uint32
U16 = mybir.dt.uint16
U8 = mybir.dt.uint8
FP8X4 = mybir.dt.float8_e4m3fn_x4
FP4X4 = mybir.dt.float4_e2m1fn_x4
ALU = mybir.AluOpType
ACT = mybir.ActivationFunctionType

P = 128
PACK = 4
PASS = P * PACK
BANK = 512
QUADS = 4
HALF = J // 2
ON_VECTOR = ((0, 0), (0, 1), (2, 1), (4, 1), (6, 1))


def tile_list_withering_trough_features_kernel(
    tc, tab_words, tab_scales, offs, pos1, pos2, pos3, pos4, w1, gain, bed, w2_words, w2_scales, w3, out
):
    nc = tc.nc
    with ExitStack() as ctx:
        lists = ctx.enter_context(tc.tile_pool(name="lists", bufs=1))
        keep = ctx.enter_context(tc.tile_pool(name="keep", bufs=1))
        psum = ctx.enter_context(tc.psum_pool(name="psum", bufs=1))

        def load_list(src, name):
            tile = lists.tile(list(src.shape), U16, name=name)
            nc.sync.dma_start(tile[:], src)
            return tile

        def bank(i):
            return psum.tile([P, BANK], F32, name="bank%d" % i, tag="bank%d" % i)

        offs_t = load_list(offs, "offs_t")

        tsc = keep.tile([P, T], U8, name="tsc", tag="tsc", align_bytes=64)
        nc.vector.memset(tsc[:].bitcast(I32), 0)
        w2s = keep.tile([P, 2, N], U8, name="w2s", align_bytes=64)
        nc.vector.memset(w2s[:].bitcast(I32), 0)

        def load_table_scales(queue):
            for q in range(QUADS):
                queue.dma_start(
                    tsc[32 * q : 32 * q + 8, :].bitcast(I32), tab_scales[:, 4 * q : 4 * q + 4, :].bitcast(I32)
                )

        gain_t = keep.tile([P, 2, PACK], F32, name="gain_t")
        nc.gpsimd.dma_start(gain_t[:], gain.rearrange("(b p t) -> p b t", p=P, t=PACK))
        for q in range(QUADS):
            nc.gpsimd.dma_start(
                w2s[32 * q : 32 * q + 4, :, :].bitcast(I32),
                w2_scales[:, 4 * q : 4 * q + 4, :].rearrange("a r n -> r a n").bitcast(I32),
            )

        def load_rows(w, a, c0, width, tag, bufs):
            raw = keep.tile([P, PACK, width], F32, name="raw", tag=tag, bufs=bufs)
            nc.sync.dma_start(
                raw[:], w[a * PASS : (a + 1) * PASS, c0 : c0 + width].rearrange("(p j) c -> p j c", j=PACK)
            )
            return raw

        bed_rows = bed.rearrange("(b p t) m -> b t p m", p=P, t=PACK)

        def load_bed(u):
            tile = keep.tile([P, S], F32, name="bed%d" % u, tag="bed%d" % u, align_bytes=64)
            nc.sync.dma_start(tile[:], bed_rows[u // PACK, u % PACK])
            return tile

        w1_raw = {}
        w1_raw[0, 0] = load_rows(w1, 0, 0, PASS, "raw", 4)
        load_table_scales(nc.sync)
        w1_raw[1, 0] = load_rows(w1, 1, 0, PASS, "raw", 4)
        tab = []
        for a in range(2):
            words = keep.tile([P, T], U32, name="tab%d" % a, tag="tab%d" % a, align_bytes=64)
            nc.sync.dma_start(words[:].bitcast(I32), tab_words[a].rearrange("p n t -> p (n t)").bitcast(I32))
            tab.append(words)

        pos1_t = load_list(pos1, "pos1_t")
        pos2_t = load_list(pos2, "pos2_t")
        bed_t = {}
        bed_t[0] = load_bed(0)
        bed_t[1] = load_bed(1)
        w1_raw[0, 1] = load_rows(w1, 0, PASS, PASS, "raw", 4)
        bed_t[2] = load_bed(2)
        w1_raw[1, 1] = load_rows(w1, 1, PASS, PASS, "raw", 4)
        bed_t[3] = load_bed(3)
        w3_raw = [load_rows(w3, 0, 0, N, "raw", 4)]
        bed_t[4] = load_bed(4)
        w3_raw.append(load_rows(w3, 1, 0, N, "raw", 4))
        bed_t[5] = load_bed(5)
        bed_t[6] = load_bed(6)

        def new_grouped(name, tag):
            return keep.tile([P, 2, PASS * PACK], BF16, name=name, tag=tag, align_bytes=64)

        def new_quant(name, width):
            codes = keep.tile([P, width], U32, name=name + "_c", align_bytes=64)
            scales = keep.tile([P, width], U8, name=name + "_s", align_bytes=64)
            return codes, scales

        def quantize(q, grouped, c0, c1):
            nc.vector.quantize_mx(
                out=q[0][:, c0:c1].bitcast(FP8X4), scales=q[1][:, c0:c1], in_=grouped[:, PACK * c0 : PACK * c1]
            )

        def deal_w1(copy, grouped, raw, m0, m1, r0):
            copy(
                grouped.rearrange("p (t m j) -> p m j t", t=PACK, j=PACK)[:, m0:m1],
                raw[:].rearrange("p j (m t) -> p m j t", t=PACK)[:, r0 : r0 + m1 - m0],
            )

        def flat(grouped):
            return grouped[:].rearrange("p a c -> p (a c)")

        w1q = [new_quant("w1q0", 2 * PASS), new_quant("w1q1", 2 * PASS)]
        g0 = new_grouped("g0", "g0")
        vs = keep.tile([P, S], U8, name="vs", align_bytes=64)
        nc.vector.tensor_copy(vs[:], tsc[:].indirect(offs_t[:]))
        for a in range(2):
            deal_w1(nc.scalar.copy, g0[:, a, :], w1_raw[a, 0], 0, P, 0)
            quantize(w1q[0], flat(g0), a * PASS, (a + 1) * PASS)
        vw = keep.tile([P, 2, S], U32, name="vw", tag="tsc", align_bytes=64)
        nc.vector.tensor_copy(vw[:, 0, :], tab[0][:].indirect(offs_t[:]))
        for c in range(2):
            nc.vector.tensor_copy(
                vw[:, 1, c * BANK : (c + 1) * BANK], tab[1][:].indirect(offs_t[:, c * 32 : (c + 1) * 32])
            )

        bed_t[7] = load_bed(7)
        w2w = keep.tile([P, 2, 2 * N], U8, name="w2w", align_bytes=64)
        nc.sync.dma_start(w2w[:].bitcast(I32), w2_words.rearrange("a p n -> p a n").bitcast(I32))
        pos3_t = load_list(pos3, "pos3_t")
        pos4_t = load_list(pos4, "pos4_t")

        acc = {}
        h = {}

        def first_pass(u, c, a):
            b, t = divmod(u, PACK)
            if a == 0:
                acc[u, c] = bank(2 * t + c)
            cols = slice(c * BANK, (c + 1) * BANK)
            rows = slice(a * PASS + t * P, a * PASS + (t + 1) * P)
            nc.tensor.matmul_mx(
                out=acc[u, c][:],
                lhsT=w1q[b][0][:, rows].bitcast(FP8X4),
                lhsT_scale=w1q[b][1][:, rows],
                rhs=vw[:, a, cols].bitcast(FP8X4),
                rhs_scale=vs[4 * a : P, cols],
                start=(a == 0),
                stop=(a == 1),
            )

        def readings(u, c):
            b, t = divmod(u, PACK)
            if c == 0:
                h[u] = keep.tile([P, S], F32, name="h", tag="h", bufs=4)
            cols = slice(c * BANK, (c + 1) * BANK)
            if (u, c) in ON_VECTOR:
                nc.vector.scalar_tensor_tensor(
                    h[u][:, cols], acc[u, c][:], gain_t[:, b, t : t + 1], bed_t[u][:, cols], ALU.mult, ALU.add
                )
            else:
                gained = keep.tile([P, BANK], F32, name="gained", tag="gained", bufs=4)
                nc.scalar.activation(gained[:], acc[u, c][:], ACT.Copy, scale=gain_t[:, b, t : t + 1])
                nc.gpsimd.tensor_tensor(h[u][:, cols], gained[:], bed_t[u][:, cols], ALU.add)

        def first_stage(u):
            for c in range(2):
                if u >= PACK:
                    first_pass(u, c, 0)
                first_pass(u, c, 1)
                readings(u, c)

        def pick_end(ends, e, u, h, j0, j1):
            pos = (pos1_t, pos2_t)[e]
            nc.vector.tensor_copy(ends[e][:, u % PACK, j0:j1], h[:].indirect(pos[:, j0 // 16 : j1 // 16]))

        def lesser(low, ends, j0, j1):
            nc.vector.tensor_tensor(
                low[:].rearrange("p (c i t) -> p c t i", i=4, t=PACK)[:, j0 // 4 : j1 // 4],
                ends[0][:].rearrange("p t (c i) -> p c t i", i=4)[:, j0 // 4 : j1 // 4],
                ends[1][:].rearrange("p t (c i) -> p c t i", i=4)[:, j0 // 4 : j1 // 4],
                ALU.min,
            )

        score = {}
        w3q = new_quant("w3q", 2 * N)

        def second_stage(a, nt, hf, lowq):
            if a == 0:
                score[nt, hf] = bank(2 * nt + hf)
            cols = slice(hf * HALF, (hf + 1) * HALF)
            nc.tensor.matmul_mx(
                out=score[nt, hf][:, 0:HALF],
                lhsT=w2w[:, a, 2 * nt * P : 2 * (nt + 1) * P].bitcast(FP4X4),
                lhsT_scale=w2s[:, a, nt * P : (nt + 1) * P],
                rhs=lowq[0][:, cols].bitcast(FP8X4),
                rhs_scale=lowq[1][:, cols],
                start=(a == 0),
                stop=False,
            )
            rows = slice(a * N + nt * P, a * N + (nt + 1) * P)
            nc.tensor.matmul_mx(
                out=score[nt, hf][:, HALF:J],
                lhsT=w3q[0][:, rows].bitcast(FP8X4),
                lhsT_scale=w3q[1][:, rows],
                rhs=lowq[0][:, cols].bitcast(FP8X4),
                rhs_scale=lowq[1][:, cols],
                start=False,
                stop=(a == 1),
            )

        def new_ends():
            return [keep.tile([P, PACK, J], F32, name="end%d" % e, tag="end%d" % e, bufs=2) for e in range(2)]

        def pick_both(ends, u, h):
            pick_end(ends, 0, u, h, 0, J)
            pick_end(ends, 1, u, h, 0, J)

        tiles = N // P
        lowq = [new_quant("lowq0", J), new_quant("lowq1", J)]
        for u in range(PACK):
            for c in range(2):
                first_pass(u, c, 0)
        for c in range(2):
            for u in range(2):
                first_pass(u, c, 1)
                readings(u, c)
        ends = new_ends()
        pick_both(ends, 0, h[0])
        first_stage(2)
        g1 = new_grouped("g1", "bed0")
        for hf in range(2):
            deal_w1(nc.scalar.copy, g1[:, 0, :], w1_raw[0, 1], 64 * hf, 64 * (hf + 1), 64 * hf)
        pick_both(ends, 1, h[1])
        first_stage(3)
        for hf in range(2):
            deal_w1(nc.scalar.copy, g1[:, 1, :], w1_raw[1, 1], 64 * hf, 64 * (hf + 1), 64 * hf)
        quantize(w1q[1], flat(g1), 0, 2 * PASS)
        pick_both(ends, 2, h[2])
        first_stage(4)
        pick_both(ends, 3, h[3])
        first_stage(5)
        low = keep.tile([P, J * PACK], BF16, name="low", tag="low", bufs=2, align_bytes=64)
        lesser(low, ends, 0, J)
        ends = new_ends()
        pick_both(ends, 4, h[4])
        quantize(lowq[0], low, 0, J)
        first_stage(6)
        pick_both(ends, 5, h[5])
        g3 = new_grouped("g3", "tab0")
        for a in range(2):
            for hf in range(2):
                nc.scalar.copy(
                    g3[:, a, :].rearrange("p (c i j) -> p c j i", i=4, j=PACK)[:, 64 * hf : 64 * (hf + 1)],
                    w3_raw[a][:].rearrange("p j (c i) -> p c j i", i=4)[:, 64 * hf : 64 * (hf + 1)],
                )
        quantize(w3q, flat(g3), 0, 2 * N)
        first_stage(7)
        pick_both(ends, 6, h[6])
        for nt in range(tiles):
            for hf in range(2):
                second_stage(0, nt, hf, lowq[0])
        low = keep.tile([P, J * PACK], BF16, name="low", tag="low", bufs=2, align_bytes=64)
        pick_end(ends, 0, 7, h[7], 0, HALF)
        pick_end(ends, 1, 7, h[7], 0, HALF)
        pick_end(ends, 0, 7, h[7], HALF, J)
        lesser(low, ends, 0, HALF)
        pick_end(ends, 1, 7, h[7], HALF, J)
        quantize(lowq[1], low, 0, HALF)
        lesser(low, ends, HALF, J)
        quantize(lowq[1], low, HALF, J)

        y = [keep.tile([P, J], F32, name="y%d" % nt) for nt in range(tiles)]
        bent = {}

        def greater(nt, hf):
            second_stage(1, nt, hf, lowq[1])
            first = keep.tile([P, HALF], F32, name="first", tag="first", bufs=4)
            nc.scalar.copy(first[:], score[nt, hf][:, 0:HALF])
            nc.vector.tensor_tensor(y[nt][:, hf * HALF : (hf + 1) * HALF], score[nt, hf][:, HALF:J], first[:], ALU.max)

        def earlier(nt):
            picked = keep.tile([P, J2], F32, name="picked", tag="picked", bufs=2)
            nc.vector.tensor_copy(picked[:], y[nt][:].indirect(pos3_t[:]))
            bent[nt] = keep.tile([P, J2], F32, name="bent", tag="bent", bufs=2)
            nc.scalar.activation(bent[nt][:], picked[:], ACT.Tanh)

        def following(nt):
            res = keep.tile([P, J2], F32, name="res%d" % nt)
            nc.vector.tensor_tensor(res[:], y[nt][:].indirect(pos4_t[:]), bent[nt][:], ALU.add)
            nc.sync.dma_start(out[nt * P : (nt + 1) * P, :], res[:])

        greater(0, 0)
        greater(1, 0)
        for step in range(tiles + 2):
            if step < tiles:
                greater(step, 1)
            if step + 2 < tiles:
                greater(step + 2, 0)
            if 1 <= step <= tiles:
                earlier(step - 1)
            if step >= 2:
                following(step - 2)
